import numpy as np, ml_dtypes
CORES = [24,27,29,56,59,61,88,91,93,120,123,125]
N = 12
KT, F = 4, 512
def setup_inputs(rng):
    return {"a": rng.standard_normal((N, 128, KT * 128), dtype=np.float32).astype(ml_dtypes.bfloat16), "w": rng.standard_normal((N, 128, KT * F), dtype=np.float32).astype(ml_dtypes.bfloat16)}
def reference(a, w):
    tot = np.zeros((128, F))
    for j in range(N):
        for t in range(KT):
            tot += a[j][:, 128 * t:128 * t + 128].astype(np.float64).T @ w[j][:, F * t:F * t + F].astype(np.float64)
    s = tot.astype(ml_dtypes.bfloat16 if a.dtype != np.float64 else np.float64)
    return {"y": np.broadcast_to(s, (N,) + s.shape)}

from concourse.bass import DstId, RemoteDMATransfer

SCRATCH = {
    "wa": ("sbuf", [128, 512], "bfloat16"),
    "aa": ("sbuf", [128, 256], "bfloat16"),
    "wb": ("sbuf", [128, 256], "bfloat16"),
    "acc": ("psum", [128, 512], "float32"),
}
SEMAPHORES = ["l_w0", "l_w2", "l_w3", "l_a01", "l_a2", "l_a3", "l_w1a", "l_w1b",
              "m0", "m1a", "m2", "m3", "cast", "arr1", "arr2", "fin", "sent", "stored"]

OWNER_CORES = (1, 2, 4, 6)
Q = 128


def _dst(topo, c):
    rid, pid, _se = topo.addr(c)
    return DstId(rid=rid, pnc=pid)


def rank_program(g, core, T, topo):
    S = T.sem
    chips = sorted(set(topo.chip(c) for c in T.cores))
    ch = topo.chip(core)
    if ch not in chips:
        return
    rank = T.rank_of(core)
    on_chip = [c for c in T.cores if topo.chip(c) == ch]

    if rank is not None:
        a, w, y = T.a, T.w, T.y
        wa, aa, wb, acc = T.wa, T.aa, T.wb, T.acc
        i = on_chip.index(core)
        g.sync.dma_start(wa[:, :], w[:, 0:512]).then_inc(S.l_w0, 16)
        g.scalar.dma_start(aa[:, :], a[:, 0:256]).then_inc(S.l_a01, 16)
        g.dma_start(wb[:, :], w[:, 512:768]).then_inc(S.l_w1a, 16)

        g.sync.wait_ge(S.m0, 1)
        g.sync.dma_start(wa[:, :], w[:, 1024:1536]).then_inc(S.l_w2, 16)
        g.scalar.wait_ge(S.m0, 1)
        g.scalar.dma_start(aa[:, 0:128], a[:, 256:384]).then_inc(S.l_a2, 16)
        g.wait_ge(S.m1a, 1)
        g.dma_start(wb[:, :], w[:, 768:1024]).then_inc(S.l_w1b, 16)

        g.sync.wait_ge(S.m2, 1)
        g.sync.dma_start(wa[:, :], w[:, 1536:2048]).then_inc(S.l_w3, 16)
        g.scalar.wait_ge(S.m2, 1)
        g.scalar.dma_start(aa[:, 0:128], a[:, 384:512]).then_inc(S.l_a3, 16)

        pe = g.tensor
        pe.wait_ge(S.l_a01, 16)
        pe.wait_ge(S.l_w0, 16)
        pe.matmul(acc[:, :], aa[:, 0:128], wa[:, :], start=True, stop=False).then_inc(S.m0, 1)
        pe.wait_ge(S.l_w1a, 16)
        pe.matmul(acc[:, 0:256], aa[:, 128:256], wb[:, :], start=False, stop=False).then_inc(S.m1a, 1)
        pe.wait_ge(S.l_a2, 16)
        pe.wait_ge(S.l_w2, 16)
        pe.matmul(acc[:, :], aa[:, 0:128], wa[:, :], start=False, stop=False).then_inc(S.m2, 1)
        pe.wait_ge(S.l_w1b, 16)
        pe.matmul(acc[:, 256:512], aa[:, 128:256], wb[:, :], start=False, stop=False).then_inc(S.m3, 1)
        pe.wait_ge(S.l_a3, 16)
        pe.wait_ge(S.l_w3, 16)
        pe.matmul(acc[:, :], aa[:, 0:128], wa[:, :], start=False, stop=True).then_inc(S.m3, 1)

        g.vector.wait_ge(S.m3, 2)
        g.vector.tensor_copy(wa[:, :], acc[:, :]).then_inc(S.cast, 1)

        g.wait_ge(S.cast, 1)
        g.remote_dma_fused(
            [RemoteDMATransfer(dst_ids=[_dst(topo, ch * 8 + OWNER_CORES[q])], dma_engine_mask=0xF << (4 * q),
                               remote_sem=S.arr1, src=wa[:, Q * q:Q * q + Q], dst=wa[:, Q * i:Q * i + Q])
             for q in range(4)],
            local_sem=S.sent)

        g.sync.wait_ge(S.fin, 64)
        g.sync.dma_start(y[:, :], wa[:, :]).then_inc(S.stored, 16)
        g.wait_ge(S.sent, 16)
        g.sync.wait_ge(S.stored, 16)
        return

    k = core % 8
    if k not in OWNER_CORES:
        return
    q = OWNER_CORES.index(k)
    wa, aa, wb = T.wa, T.aa, T.wb
    mine = [wa[:, Q * i:Q * i + Q] for i in range(len(on_chip))]
    far = [aa[:, 0:Q], aa[:, Q:2 * Q], wb[:, 0:Q]]
    ci = chips.index(ch)
    others = [cj for cj in range(4) if cj != ci]
    g.wait_ge(S.arr1, 4 * len(on_chip))
    g.remote_dma_fused(
        [RemoteDMATransfer(dst_ids=[_dst(topo, chips[cj] * 8 + k) for cj in others], dma_engine_mask=0x00FF,
                           remote_sem=S.arr2, srcs=mine, dsts=[far[(ci - cj - 1) % 4] for cj in others], alu_op=1)],
        local_sem=S.sent)
    g.wait_ge(S.arr2, 8 * 3)
    g.remote_dma_fused(
        [RemoteDMATransfer(dst_ids=[_dst(topo, c) for c in on_chip], dma_engine_mask=0xFFFF,
                           remote_sem=S.fin, srcs=mine + far, dsts=[wa[:, Q * q:Q * q + Q] for _c in on_chip],
                           alu_op=1)],
        local_sem=S.sent)
    g.wait_ge(S.sent, 8 + 16)
